import numpy as np
import ml_dtypes


def mxq(x, axis, fmt="e4m3"):
    dtype, down = {"e4m3": (ml_dtypes.float8_e4m3fn, 7), "e5m2": (ml_dtypes.float8_e5m2, 14)}[fmt]
    v = np.moveaxis(np.asarray(x, np.float32).astype(ml_dtypes.bfloat16).astype(np.float64), axis, -1)
    blocks = v.reshape(v.shape[:-1] + (-1, 32))
    amax = np.abs(blocks).max(-1, keepdims=True)
    byte = np.maximum(np.where(amax > 0, np.frexp(amax)[1] - 1 + 127, 0) - down, 1)
    scale = np.exp2(byte - 127.0)
    codes = (blocks / scale).astype(np.float32).astype(dtype).astype(np.float64)
    return np.moveaxis((codes * scale).reshape(v.shape), -1, axis)


WIDE = False


def mx_kscale(k):
    if not WIDE:
        return np.ones(k)
    levels = np.array([10, -10, 5, -5, 0])
    if k % 512:
        return np.exp2(np.random.permutation(np.resize(levels, k // 32))).repeat(32)
    a = np.empty((k // 512, 16))
    for p in range(k // 512):
        a[p, :8] = np.random.permutation(np.resize(levels, 8))
        for g in range(8):
            far = levels[np.abs(levels - a[p, g]) >= 10]
            a[p, g + 8] = far[np.random.randint(len(far))]
    return np.exp2(a.ravel()).repeat(32)


def f64(x):
    return np.asarray(x).astype(np.float64)


def striped(idx):
    return np.tile(np.asarray(idx).reshape(-1, 16).T, (8, 1)).astype(np.uint16)


def unstriped(offs):
    return offs[:16].T.reshape(-1).astype(np.int64)


E2M1 = np.array([0.0, 0.5, 1.0, 1.5, 2.0, 3.0, 4.0, 6.0, -0.0, -0.5, -1.0, -1.5, -2.0, -3.0, -4.0, -6.0])


def pack_weight(w, fmt):
    k, n = w.shape
    w = f64(np.asarray(w, np.float32).astype(ml_dtypes.bfloat16)).reshape(k // 32, 32, n)
    amax = np.abs(w).max(1)
    if fmt == "e4m3":
        byte = np.frexp(amax)[1] - 1 + 127 - 7
    else:
        mant, ex = np.frexp(amax / 6.0)
        byte = np.where(mant > 0.5, ex, ex - 1) + 127
    byte = np.clip(np.where(amax > 0, byte, 1), 1, 254)
    scaled = (w * np.exp2(127.0 - byte)[:, None, :]).reshape(k, n).astype(np.float32)
    by_word = np.ascontiguousarray(scaled.reshape(k // 512, 128, 4, n).transpose(0, 1, 3, 2))
    if fmt == "e4m3":
        words = by_word.astype(ml_dtypes.float8_e4m3fn).view(np.uint8)
    else:
        c = by_word.astype(ml_dtypes.float4_e2m1fn).view(np.uint8) & 0xF
        words = (c[..., 0::2] | (c[..., 1::2] << 4)).reshape(k // 512, 128, 2 * n)
    return np.ascontiguousarray(words), np.ascontiguousarray(byte.astype(np.uint8).reshape(k // 512, 16, n))


def unpack_weight(words, scales, fmt):
    g, _, n = scales.shape
    words = np.ascontiguousarray(words).reshape(g, 128, n, -1)
    if fmt == "e4m3":
        vals = words.view(ml_dtypes.float8_e4m3fn).astype(np.float64)
    else:
        nib = np.empty((g, 128, n, 4), np.uint8)
        nib[..., 0::2] = words & 0xF
        nib[..., 1::2] = words >> 4
        vals = E2M1[nib]
    vals = vals * np.repeat(np.exp2(scales.astype(np.float64) - 127.0), 8, axis=1)[..., None]
    return vals.transpose(0, 1, 3, 2).reshape(g * 512, n)


D, K, T, U, I, J, C = 512, 512, 2048, 1024, 512, 512, 256


def setup_inputs():
    n = np.random.standard_normal
    idx = np.random.permutation(T)[:I]
    idx2 = np.random.permutation(U)[:J]
    idx3 = np.random.permutation(J)[:C]
    fd = mx_kscale(D)
    fk = mx_kscale(K)
    pagesp = pack_weight(n((D, T)) / fd[:, None], "e2m1")
    wap = pack_weight(n((D, K)) * 1.0 / np.sqrt(D) * fd[:, None] * fk, "e4m3")
    notesp = pack_weight(n((D, U)) / fd[:, None], "e4m3")
    wbp = pack_weight(n((D, K)) * 1.0 / np.sqrt(D) * fd[:, None], "e2m1")
    return {
        "pages_words": pagesp[0],
        "pages_scales": pagesp[1],
        "wa_words": wap[0],
        "wa_scales": wap[1],
        "notes_words": notesp[0],
        "notes_scales": notesp[1],
        "wb_words": wbp[0],
        "wb_scales": wbp[1],
        "kf": (np.random.uniform(0.03, 0.09, (K, 1)) / fk[:, None]).astype(np.float32),
        "offs": striped(idx),
        "offs2": striped(idx2),
        "offs3": striped(idx3),
    }


def reference(pages_words, pages_scales, wa_words, wa_scales, notes_words, notes_scales, wb_words, wb_scales, kf, offs, offs2, offs3):
    idx = unstriped(offs)
    idx2 = unstriped(offs2)
    idx3 = unstriped(offs3)
    pagesu = unpack_weight(pages_words, pages_scales, "e2m1")
    wau = unpack_weight(wa_words, wa_scales, "e4m3")
    notesu = unpack_weight(notes_words, notes_scales, "e4m3")
    wbu = unpack_weight(wb_words, wb_scales, "e2m1")
    pagesidxg = pagesu[:, idx]
    z = wau.T @ pagesidxg
    notesidx2g = notesu[:, idx2]
    h2 = wbu.T @ notesidx2g
    h3 = h2 * f64(kf)
    zq = mxq(z, 0, "e4m3")
    h3q = mxq(h3, 0, "e4m3")
    s = zq.T @ h3q
    ts = np.max(s, axis=1, keepdims=True)
    y = np.exp(s[:, idx3] - ts)
    return y

@@ -1,0 +1,176 @@
+from contextlib import ExitStack
+
+import concourse.mybir as mybir
+from concourse.masks import make_identity
+
+D, K, T, U, I, J, C = 512, 512, 2048, 1024, 512, 512, 256
+FLOPS = 2 * D * K * I + 2 * D * K * J + 2 * K * I * J
+
+F32 = mybir.dt.float32
+BF16 = mybir.dt.bfloat16
+I32 = mybir.dt.int32
+U32 = mybir.dt.uint32
+U16 = mybir.dt.uint16
+U8 = mybir.dt.uint8
+FP8X4 = mybir.dt.float8_e4m3fn_x4
+FP4X4 = mybir.dt.float4_e2m1fn_x4
+ALU = mybir.AluOpType
+ACT = mybir.ActivationFunctionType
+
+P = 128
+PLACES = 4
+RUN = 8
+CHUNK = 128
+CHUNKS = 4
+
+
+def load_scale_rows(queue, plane, scales):
+    rows = scales[0].bitcast(I32)
+    for q in range(4):
+        queue.dma_start(out=plane[32 * q : 32 * q + 4, :].bitcast(I32), in_=rows[4 * q : 4 * q + 4, :])
+
+
+def deal_columns(nc, dealt, natural):
+    nc.scalar.copy(
+        dealt[:].bitcast(U32).rearrange("p (t g r) -> p t g r", t=PLACES, g=16),
+        natural[:].bitcast(U32).rearrange("p (g t r) -> p t g r", t=PLACES, g=16),
+    )
+
+
+def tile_attend_matchtable_kernel(
+    tc, pages_words, pages_scales, wa_words, wa_scales, notes_words, notes_scales, wb_words, wb_scales, kf, offs, offs2, offs3, out
+):
+    nc = tc.nc
+    with ExitStack() as ctx:
+        sb = ctx.enter_context(tc.tile_pool(name="sb", bufs=1))
+        ps = ctx.enter_context(tc.psum_pool(name="ps", bufs=1))
+
+        page_list = sb.tile([P, I // 16], U16, name="page_list")
+        note_list = sb.tile([P, J // 16], U16, name="note_list")
+        col_list = sb.tile([P, C // 16], U16, name="col_list")
+        page_w = sb.tile([P, T], U16, name="page_w", align_bytes=64)
+        page_s = sb.tile([P, T], U8, name="page_s", align_bytes=64)
+        note_w = sb.tile([P, U], U32, name="note_w", align_bytes=64)
+        note_s = sb.tile([P, U], U8, name="note_s", align_bytes=64)
+        wa_w = sb.tile([P, K], U32, name="wa_w", align_bytes=64)
+        wa_s = sb.tile([P, K], U8, name="wa_s", align_bytes=64)
+        wb_w = sb.tile([P, 2 * K], U8, name="wb_w", align_bytes=64)
+        wb_s = sb.tile([P, K], U8, name="wb_s", align_bytes=64)
+        factor = sb.tile([P, PLACES], F32, name="factor")
+        factor_rows = sb.tile([P, P], F32, name="factor_rows")
+        identity = sb.tile([P, P], F32, name="identity")
+
+        nc.vector.memset(note_s[:].bitcast(I32), 0)
+        nc.vector.memset(wb_s[:].bitcast(I32), 0)
+        nc.vector.memset(page_s[:].bitcast(I32), 0)
+        nc.gpsimd.memset(factor_rows[:], 0.0)
+        nc.gpsimd.memset(wa_s[:].bitcast(I32), 0)
+
+        nc.sync.dma_start(note_list[:], offs2)
+        load_scale_rows(nc.scalar, note_s, notes_scales)
+        nc.sync.dma_start(out=note_w[:].bitcast(I32), in_=notes_words[0].rearrange("p n t -> p (n t)").bitcast(I32))
+        nc.sync.dma_start(out=wb_w[:].bitcast(I32), in_=wb_words[0].bitcast(I32))
+        nc.sync.dma_start(page_list[:], offs)
+        nc.gpsimd.dma_start(
+            out=factor_rows[0:PLACES, :].rearrange("t (g r) -> t g r", r=RUN),
+            in_=kf.rearrange("(g t r) o -> t g (r o)", t=PLACES, r=RUN),
+        )
+        load_scale_rows(nc.sync, wb_s, wb_scales)
+        nc.sync.dma_start(out=page_w[:].bitcast(I32), in_=pages_words[0].bitcast(I32))
+        load_scale_rows(nc.sync, page_s, pages_scales)
+        nc.sync.dma_start(out=wa_w[:].bitcast(I32), in_=wa_words[0].rearrange("p n t -> p (n t)").bitcast(I32))
+        make_identity(nc, identity[:])
+        load_scale_rows(nc.sync, wa_s, wa_scales)
+        nc.sync.dma_start(col_list[:], offs3)
+
+        factor_bank = ps.tile([P, PLACES * CHUNK], F32, name="factor_bank", tag="z3")
+        nc.tensor.transpose(factor_bank[:, 0:P], factor_rows[:], identity[:])
+        nc.scalar.copy(factor[:], factor_bank[:, 0:PLACES])
+
+        wb_wd = sb.tile([P, 2 * K], U8, name="wb_wd", align_bytes=64)
+        wb_sd = sb.tile([P, K], U8, name="wb_sd", align_bytes=64)
+        wa_wd = sb.tile([P, K], U32, name="wa_wd", align_bytes=64)
+        wa_sd = sb.tile([P, K], U8, name="wa_sd", align_bytes=64)
+        deal_columns(nc, wb_wd, wb_w)
+        deal_columns(nc, wb_sd, wb_s)
+        deal_columns(nc, wa_wd, wa_w)
+        deal_columns(nc, wa_sd, wa_s)
+
+        note_wg = sb.tile([P, J], U32, name="note_wg", align_bytes=64)
+        note_sg = sb.tile([P, J], U8, name="note_sg", align_bytes=64)
+        page_wg = sb.tile([P, I], U16, name="page_wg", align_bytes=64)
+        page_sg = sb.tile([P, I], U8, name="page_sg", align_bytes=64)
+        nc.vector.tensor_copy(note_sg[:], note_s[:].indirect(note_list[:]))
+        nc.vector.tensor_copy(note_wg[:], note_w[:].indirect(note_list[:]))
+        nc.vector.tensor_copy(page_wg[:], page_w[:].indirect(page_list[:]))
+        nc.vector.tensor_copy(page_sg[:], page_s[:].indirect(page_list[:]))
+
+        h_bf = sb.tile([P, J * PLACES], BF16, name="h_bf", align_bytes=64)
+        h_q = sb.tile([P, J], U32, name="h_q", align_bytes=64)
+        h_qs = sb.tile([P, J], U8, name="h_qs", align_bytes=64)
+        factor_b = factor[:].unsqueeze(1).to_broadcast([P, CHUNK, PLACES])
+        for c in range(CHUNKS):
+            cols = slice(c * CHUNK, (c + 1) * CHUNK)
+            bank = ps.tile([P, PLACES * CHUNK], F32, name="h_bank", tag=f"hs{c}")
+            for t in range(PLACES):
+                nc.tensor.matmul_mx(
+                    out=bank[:, t * CHUNK : (t + 1) * CHUNK],
+                    lhsT=wb_wd[:, 2 * P * t : 2 * P * (t + 1)].bitcast(FP4X4),
+                    lhsT_scale=wb_sd[:, P * t : P * (t + 1)],
+                    rhs=note_wg[:, cols].bitcast(FP8X4),
+                    rhs_scale=note_sg[:, cols],
+                    start=True,
+                    stop=True,
+                )
+            nc.vector.tensor_tensor(
+                h_bf[:, c * CHUNK * PLACES : (c + 1) * CHUNK * PLACES].rearrange("p (n t) -> p n t", t=PLACES),
+                bank[:].rearrange("p (t n) -> p n t", t=PLACES),
+                factor_b,
+                ALU.mult,
+            )
+        nc.vector.quantize_mx(out=h_q[:].bitcast(FP8X4), scales=h_qs[:], in_=h_bf[:])
+
+        z_bf = []
+        for c in range(CHUNKS):
+            cols = slice(c * CHUNK, (c + 1) * CHUNK)
+            bank = ps.tile([P, PLACES * CHUNK], F32, name="z_bank", tag=f"z{c}")
+            for t in range(PLACES):
+                nc.tensor.matmul_mx(
+                    out=bank[:, t * CHUNK : (t + 1) * CHUNK],
+                    lhsT=wa_wd[:, P * t : P * (t + 1)].bitcast(FP8X4),
+                    lhsT_scale=wa_sd[:, P * t : P * (t + 1)],
+                    rhs=page_wg[:, cols].bitcast(FP4X4),
+                    rhs_scale=page_sg[:, cols],
+                    start=True,
+                    stop=True,
+                )
+            zc = sb.tile([P, CHUNK * PLACES], BF16, name=f"z_bf{c}", align_bytes=64)
+            nc.scalar.activation(
+                zc[:].rearrange("p (n t) -> p n t", t=PLACES),
+                bank[:].rearrange("p (t n) -> p n t", t=PLACES),
+                ACT.Copy,
+            )
+            z_bf.append(zc)
+
+        for c in range(CHUNKS):
+            z_q = sb.tile([P, CHUNK], U32, name=f"z_q{c}", align_bytes=64)
+            z_qs = sb.tile([P, CHUNK], U8, name=f"z_qs{c}", align_bytes=64)
+            nc.vector.quantize_mx(out=z_q[:].bitcast(FP8X4), scales=z_qs[:], in_=z_bf[c][:])
+            bank = ps.tile([P, J], F32, name="s_bank", tag=f"hs{c}")
+            nc.tensor.matmul_mx(
+                out=bank[:],
+                lhsT=z_q[:].bitcast(FP8X4),
+                lhsT_scale=z_qs[:],
+                rhs=h_q[:].bitcast(FP8X4),
+                rhs_scale=h_qs[:],
+                start=True,
+                stop=True,
+            )
+            table = sb.tile([P, J], F32, name=f"table{c}")
+            top = sb.tile([P, 1], F32, name=f"top{c}")
+            neg_top = sb.tile([P, 1], F32, name=f"neg_top{c}")
+            picked = sb.tile([P, C], F32, name=f"picked{c}")
+            nc.vector.tensor_scalar(table[:], bank[:], 1.0, None, ALU.mult, ALU.max, accum_out=top[:])
+            nc.gpsimd.tensor_scalar(neg_top[:], top[:], -1.0, 0.0, ALU.mult, ALU.add)
+            nc.scalar.activation(picked[:], table[:].indirect(col_list[:]), ACT.Exp, bias=neg_top[:])
+            nc.sync.dma_start(out=out[c * P : (c + 1) * P, :], in_=picked[:])

@@ -26,8 +26,8 @@ CHUNKS = 4
 
 def load_scale_rows(queue, plane, scales):
     rows = scales[0].bitcast(I32)
-    for q in range(4):
-        queue.dma_start(out=plane[32 * q : 32 * q + 4, :].bitcast(I32), in_=rows[4 * q : 4 * q + 4, :])
+    for r in range(4):
+        queue.dma_start(out=plane[r:P:32, :].bitcast(I32), in_=rows[r:16:4, :])
 
 
 def deal_columns(nc, dealt, natural):
@@ -49,7 +49,7 @@ def tile_attend_matchtable_kernel(
         note_list = sb.tile([P, J // 16], U16, name="note_list")
         col_list = sb.tile([P, C // 16], U16, name="col_list")
         page_w = sb.tile([P, T], U16, name="page_w", align_bytes=64)
-        page_s = sb.tile([P, T], U8, name="page_s", align_bytes=64)
+        page_s = sb.tile([P, T], U8, name="page_s", tag="page_s_then_h", align_bytes=64)
         note_w = sb.tile([P, U], U32, name="note_w", align_bytes=64)
         note_s = sb.tile([P, U], U8, name="note_s", align_bytes=64)
         wa_w = sb.tile([P, K], U32, name="wa_w", align_bytes=64)
@@ -61,25 +61,25 @@ def tile_attend_matchtable_kernel(
         identity = sb.tile([P, P], F32, name="identity")
 
         nc.vector.memset(note_s[:].bitcast(I32), 0)
+        nc.vector.memset(factor_rows[:], 0.0)
         nc.vector.memset(wb_s[:].bitcast(I32), 0)
         nc.vector.memset(page_s[:].bitcast(I32), 0)
-        nc.gpsimd.memset(factor_rows[:], 0.0)
-        nc.gpsimd.memset(wa_s[:].bitcast(I32), 0)
+        nc.vector.memset(wa_s[:].bitcast(I32), 0)
 
+        nc.gpsimd.dma_start(out=wb_w[:].bitcast(I32), in_=wb_words[0].bitcast(I32))
+        nc.gpsimd.dma_start(out=wa_w[:].bitcast(I32), in_=wa_words[0].rearrange("p n t -> p (n t)").bitcast(I32))
+        make_identity(nc, identity[:])
         nc.sync.dma_start(note_list[:], offs2)
-        load_scale_rows(nc.scalar, note_s, notes_scales)
         nc.sync.dma_start(out=note_w[:].bitcast(I32), in_=notes_words[0].rearrange("p n t -> p (n t)").bitcast(I32))
-        nc.sync.dma_start(out=wb_w[:].bitcast(I32), in_=wb_words[0].bitcast(I32))
+        load_scale_rows(nc.sync, note_s, notes_scales)
         nc.sync.dma_start(page_list[:], offs)
-        nc.gpsimd.dma_start(
+        nc.sync.dma_start(out=page_w[:].bitcast(I32), in_=pages_words[0].bitcast(I32))
+        nc.sync.dma_start(
             out=factor_rows[0:PLACES, :].rearrange("t (g r) -> t g r", r=RUN),
             in_=kf.rearrange("(g t r) o -> t g (r o)", t=PLACES, r=RUN),
         )
         load_scale_rows(nc.sync, wb_s, wb_scales)
-        nc.sync.dma_start(out=page_w[:].bitcast(I32), in_=pages_words[0].bitcast(I32))
         load_scale_rows(nc.sync, page_s, pages_scales)
-        nc.sync.dma_start(out=wa_w[:].bitcast(I32), in_=wa_words[0].rearrange("p n t -> p (n t)").bitcast(I32))
-        make_identity(nc, identity[:])
         load_scale_rows(nc.sync, wa_s, wa_scales)
         nc.sync.dma_start(col_list[:], offs3)
 
@@ -92,29 +92,30 @@ def tile_attend_matchtable_kernel(
         wa_wd = sb.tile([P, K], U32, name="wa_wd", align_bytes=64)
         wa_sd = sb.tile([P, K], U8, name="wa_sd", align_bytes=64)
         deal_columns(nc, wb_wd, wb_w)
-        deal_columns(nc, wb_sd, wb_s)
         deal_columns(nc, wa_wd, wa_w)
+        deal_columns(nc, wb_sd, wb_s)
         deal_columns(nc, wa_sd, wa_s)
 
         note_wg = sb.tile([P, J], U32, name="note_wg", align_bytes=64)
         note_sg = sb.tile([P, J], U8, name="note_sg", align_bytes=64)
         page_wg = sb.tile([P, I], U16, name="page_wg", align_bytes=64)
         page_sg = sb.tile([P, I], U8, name="page_sg", align_bytes=64)
-        nc.vector.tensor_copy(note_sg[:], note_s[:].indirect(note_list[:]))
         nc.vector.tensor_copy(note_wg[:], note_w[:].indirect(note_list[:]))
+        nc.vector.tensor_copy(note_sg[:], note_s[:].indirect(note_list[:]))
         nc.vector.tensor_copy(page_wg[:], page_w[:].indirect(page_list[:]))
         nc.vector.tensor_copy(page_sg[:], page_s[:].indirect(page_list[:]))
 
-        h_bf = sb.tile([P, J * PLACES], BF16, name="h_bf", align_bytes=64)
+        h_planes = sb.tile([P, PLACES, J], BF16, name="h_planes", align_bytes=64)
+        h_bf = sb.tile([P, J * PLACES], BF16, name="h_bf", tag="page_s_then_h", align_bytes=64)
         h_q = sb.tile([P, J], U32, name="h_q", align_bytes=64)
         h_qs = sb.tile([P, J], U8, name="h_qs", align_bytes=64)
-        factor_b = factor[:].unsqueeze(1).to_broadcast([P, CHUNK, PLACES])
-        for c in range(CHUNKS):
-            cols = slice(c * CHUNK, (c + 1) * CHUNK)
-            bank = ps.tile([P, PLACES * CHUNK], F32, name="h_bank", tag=f"hs{c}")
+        h_banks = [ps.tile([P, J], F32, name="h_bank", tag=f"hs{t}") for t in range(PLACES)]
+        half = J // 2
+        for a in range(2):
+            cols = slice(a * half, (a + 1) * half)
             for t in range(PLACES):
                 nc.tensor.matmul_mx(
-                    out=bank[:, t * CHUNK : (t + 1) * CHUNK],
+                    out=h_banks[t][:, cols],
                     lhsT=wb_wd[:, 2 * P * t : 2 * P * (t + 1)].bitcast(FP4X4),
                     lhsT_scale=wb_sd[:, P * t : P * (t + 1)],
                     rhs=note_wg[:, cols].bitcast(FP8X4),
@@ -122,13 +123,18 @@ def tile_attend_matchtable_kernel(
                     start=True,
                     stop=True,
                 )
-            nc.vector.tensor_tensor(
-                h_bf[:, c * CHUNK * PLACES : (c + 1) * CHUNK * PLACES].rearrange("p (n t) -> p n t", t=PLACES),
-                bank[:].rearrange("p (t n) -> p n t", t=PLACES),
-                factor_b,
-                ALU.mult,
+                nc.scalar.activation(h_planes[:, t, cols], h_banks[t][:, cols], ACT.Copy, scale=factor[:, t : t + 1])
+        for a in range(2):
+            cols = slice(a * half, (a + 1) * half)
+            words = slice(a * half * PLACES, (a + 1) * half * PLACES)
+            nc.vector.tensor_copy(
+                h_bf[:, words].rearrange("p (c i t) -> p c t i", i=4, t=PLACES),
+                h_planes[:, :, cols].rearrange("p t (c i) -> p c t i", i=4),
             )
-        nc.vector.quantize_mx(out=h_q[:].bitcast(FP8X4), scales=h_qs[:], in_=h_bf[:])
+        for a in range(2):
+            cols = slice(a * half, (a + 1) * half)
+            words = slice(a * half * PLACES, (a + 1) * half * PLACES)
+            nc.vector.quantize_mx(out=h_q[:, cols].bitcast(FP8X4), scales=h_qs[:, cols], in_=h_bf[:, words])
 
         z_bf = []
         for c in range(CHUNKS):
@@ -144,7 +150,7 @@ def tile_attend_matchtable_kernel(
                     start=True,
                     stop=True,
                 )
-            zc = sb.tile([P, CHUNK * PLACES], BF16, name=f"z_bf{c}", align_bytes=64)
+            zc = sb.tile([P, CHUNK * PLACES], BF16, name=f"z_bf{c}", tag=f"z_then_table{c}", align_bytes=64)
             nc.scalar.activation(
                 zc[:].rearrange("p (n t) -> p n t", t=PLACES),
                 bank[:].rearrange("p (t n) -> p n t", t=PLACES),
@@ -152,10 +158,15 @@ def tile_attend_matchtable_kernel(
             )
             z_bf.append(zc)
 
+        z_mx = []
         for c in range(CHUNKS):
             z_q = sb.tile([P, CHUNK], U32, name=f"z_q{c}", align_bytes=64)
             z_qs = sb.tile([P, CHUNK], U8, name=f"z_qs{c}", align_bytes=64)
             nc.vector.quantize_mx(out=z_q[:].bitcast(FP8X4), scales=z_qs[:], in_=z_bf[c][:])
+            z_mx.append((z_q, z_qs))
+
+        for c in range(CHUNKS):
+            z_q, z_qs = z_mx[c]
             bank = ps.tile([P, J], F32, name="s_bank", tag=f"hs{c}")
             nc.tensor.matmul_mx(
                 out=bank[:],
@@ -166,7 +177,7 @@ def tile_attend_matchtable_kernel(
                 start=True,
                 stop=True,
             )
-            table = sb.tile([P, J], F32, name=f"table{c}")
+            table = sb.tile([P, J], F32, name=f"table{c}", tag=f"z_then_table{CHUNKS - 1 - c}", align_bytes=64)
             top = sb.tile([P, 1], F32, name=f"top{c}")
             neg_top = sb.tile([P, 1], F32, name=f"neg_top{c}")
             picked = sb.tile([P, C], F32, name=f"picked{c}")

@@ -20,20 +20,26 @@ ACT = mybir.ActivationFunctionType
 P = 128
 PLACES = 4
 RUN = 8
-CHUNK = 128
-CHUNKS = 4
+BLOCKS = K // (PLACES * RUN)
+QUADRANT = 32
+SCALE_ROWS = 4
+LIST_ROWS = 16
+TILES = I // P
+HALF = J // 2
+LINE = 4
+ALIGN = 64
 
 
-def load_scale_rows(queue, plane, scales):
+def load_scale_rows(nc, scale_tile, scales):
     rows = scales[0].bitcast(I32)
-    for r in range(4):
-        queue.dma_start(out=plane[r:P:32, :].bitcast(I32), in_=rows[r:16:4, :])
+    for r in range(SCALE_ROWS):
+        nc.sync.dma_start(out=scale_tile[r:P:QUADRANT, :].bitcast(I32), in_=rows[r:BLOCKS:SCALE_ROWS, :])
 
 
-def deal_columns(nc, dealt, natural):
-    nc.scalar.copy(
-        dealt[:].bitcast(U32).rearrange("p (t g r) -> p t g r", t=PLACES, g=16),
-        natural[:].bitcast(U32).rearrange("p (g t r) -> p t g r", t=PLACES, g=16),
+def dealt_views(dealt, natural, dtype):
+    return (
+        dealt[:].bitcast(dtype).rearrange("p (t g r) -> p t g r", t=PLACES, g=BLOCKS),
+        natural[:].bitcast(dtype).rearrange("p (g t r) -> p t g r", t=PLACES, g=BLOCKS),
     )
 
 
@@ -45,17 +51,17 @@ def tile_attend_matchtable_kernel(
         sb = ctx.enter_context(tc.tile_pool(name="sb", bufs=1))
         ps = ctx.enter_context(tc.psum_pool(name="ps", bufs=1))
 
-        page_list = sb.tile([P, I // 16], U16, name="page_list")
-        note_list = sb.tile([P, J // 16], U16, name="note_list")
-        col_list = sb.tile([P, C // 16], U16, name="col_list")
-        page_w = sb.tile([P, T], U16, name="page_w", align_bytes=64)
-        page_s = sb.tile([P, T], U8, name="page_s", tag="page_s_then_h", align_bytes=64)
-        note_w = sb.tile([P, U], U32, name="note_w", align_bytes=64)
-        note_s = sb.tile([P, U], U8, name="note_s", align_bytes=64)
-        wa_w = sb.tile([P, K], U32, name="wa_w", align_bytes=64)
-        wa_s = sb.tile([P, K], U8, name="wa_s", align_bytes=64)
-        wb_w = sb.tile([P, 2 * K], U8, name="wb_w", align_bytes=64)
-        wb_s = sb.tile([P, K], U8, name="wb_s", align_bytes=64)
+        page_list = sb.tile([P, I // LIST_ROWS], U16, name="page_list")
+        note_list = sb.tile([P, J // LIST_ROWS], U16, name="note_list")
+        col_list = sb.tile([P, C // LIST_ROWS], U16, name="col_list")
+        page_w = sb.tile([P, T], U16, name="page_w", align_bytes=ALIGN)
+        page_s = sb.tile([P, T], U8, name="page_s", tag="page_s_then_h_bf", align_bytes=ALIGN)
+        note_w = sb.tile([P, U], U32, name="note_w", align_bytes=ALIGN)
+        note_s = sb.tile([P, U], U8, name="note_s", align_bytes=ALIGN)
+        wa_w = sb.tile([P, K], U32, name="wa_w", align_bytes=ALIGN)
+        wa_s = sb.tile([P, K], U8, name="wa_s", tag="wa_s_then_h_q", align_bytes=ALIGN)
+        wb_w = sb.tile([P, 2 * K], U8, name="wb_w", align_bytes=ALIGN)
+        wb_s = sb.tile([P, K], U8, name="wb_s", align_bytes=ALIGN)
         factor = sb.tile([P, PLACES], F32, name="factor")
         factor_rows = sb.tile([P, P], F32, name="factor_rows")
         identity = sb.tile([P, P], F32, name="identity")
@@ -71,105 +77,104 @@ def tile_attend_matchtable_kernel(
         make_identity(nc, identity[:])
         nc.sync.dma_start(note_list[:], offs2)
         nc.sync.dma_start(out=note_w[:].bitcast(I32), in_=notes_words[0].rearrange("p n t -> p (n t)").bitcast(I32))
-        load_scale_rows(nc.sync, note_s, notes_scales)
+        load_scale_rows(nc, note_s, notes_scales)
         nc.sync.dma_start(page_list[:], offs)
         nc.sync.dma_start(out=page_w[:].bitcast(I32), in_=pages_words[0].bitcast(I32))
         nc.sync.dma_start(
             out=factor_rows[0:PLACES, :].rearrange("t (g r) -> t g r", r=RUN),
             in_=kf.rearrange("(g t r) o -> t g (r o)", t=PLACES, r=RUN),
         )
-        load_scale_rows(nc.sync, wb_s, wb_scales)
-        load_scale_rows(nc.sync, page_s, pages_scales)
-        load_scale_rows(nc.sync, wa_s, wa_scales)
+        load_scale_rows(nc, wb_s, wb_scales)
+        load_scale_rows(nc, page_s, pages_scales)
+        load_scale_rows(nc, wa_s, wa_scales)
         nc.sync.dma_start(col_list[:], offs3)
 
-        factor_bank = ps.tile([P, PLACES * CHUNK], F32, name="factor_bank", tag="z3")
+        factor_bank = ps.tile([P, PLACES * P], F32, name="factor_bank", tag=f"z{TILES - 1}")
         nc.tensor.transpose(factor_bank[:, 0:P], factor_rows[:], identity[:])
         nc.scalar.copy(factor[:], factor_bank[:, 0:PLACES])
 
-        wb_wd = sb.tile([P, 2 * K], U8, name="wb_wd", align_bytes=64)
-        wb_sd = sb.tile([P, K], U8, name="wb_sd", align_bytes=64)
-        wa_wd = sb.tile([P, K], U32, name="wa_wd", align_bytes=64)
-        wa_sd = sb.tile([P, K], U8, name="wa_sd", align_bytes=64)
-        deal_columns(nc, wb_wd, wb_w)
-        deal_columns(nc, wa_wd, wa_w)
-        deal_columns(nc, wb_sd, wb_s)
-        deal_columns(nc, wa_sd, wa_s)
+        wb_wd = sb.tile([P, 2 * K], U8, name="wb_wd", align_bytes=ALIGN)
+        wb_sd = sb.tile([P, K], U8, name="wb_sd", align_bytes=ALIGN)
+        wa_wd = sb.tile([P, K], U32, name="wa_wd", align_bytes=ALIGN)
+        wa_sd = sb.tile([P, K], U8, name="wa_sd", align_bytes=ALIGN)
+        nc.scalar.copy(*dealt_views(wb_wd, wb_w, U32))
+        nc.scalar.copy(*dealt_views(wa_wd, wa_w, U32))
+        nc.scalar.copy(*dealt_views(wb_sd, wb_s, U32))
 
-        note_wg = sb.tile([P, J], U32, name="note_wg", align_bytes=64)
-        note_sg = sb.tile([P, J], U8, name="note_sg", align_bytes=64)
-        page_wg = sb.tile([P, I], U16, name="page_wg", align_bytes=64)
-        page_sg = sb.tile([P, I], U8, name="page_sg", align_bytes=64)
+        note_wg = sb.tile([P, J], U32, name="note_wg", align_bytes=ALIGN)
+        note_sg = sb.tile([P, J], U8, name="note_sg", align_bytes=ALIGN)
+        page_wg = sb.tile([P, I], U16, name="page_wg", align_bytes=ALIGN)
+        page_sg = sb.tile([P, I], U8, name="page_sg", align_bytes=ALIGN)
         nc.vector.tensor_copy(note_wg[:], note_w[:].indirect(note_list[:]))
         nc.vector.tensor_copy(note_sg[:], note_s[:].indirect(note_list[:]))
         nc.vector.tensor_copy(page_wg[:], page_w[:].indirect(page_list[:]))
         nc.vector.tensor_copy(page_sg[:], page_s[:].indirect(page_list[:]))
 
-        h_planes = sb.tile([P, PLACES, J], BF16, name="h_planes", align_bytes=64)
-        h_bf = sb.tile([P, J * PLACES], BF16, name="h_bf", tag="page_s_then_h", align_bytes=64)
-        h_q = sb.tile([P, J], U32, name="h_q", align_bytes=64)
-        h_qs = sb.tile([P, J], U8, name="h_qs", align_bytes=64)
-        h_banks = [ps.tile([P, J], F32, name="h_bank", tag=f"hs{t}") for t in range(PLACES)]
-        half = J // 2
+        nc.vector.tensor_copy(*dealt_views(wa_sd, wa_s, I32))
+
+        h_bf = sb.tile([P, J * PLACES], BF16, name="h_bf", tag="page_s_then_h_bf", align_bytes=ALIGN)
+        h_q = sb.tile([P, J], U32, name="h_q", tag="wa_s_then_h_q", align_bytes=ALIGN)
+        h_qs = sb.tile([P, J], U8, name="h_qs", align_bytes=ALIGN)
+        h_banks = [ps.tile([P, J], F32, name="h_bank", tag=f"h_then_s{t}") for t in range(PLACES)]
+        h_places = [sb.tile([P, PLACES, HALF], BF16, name=f"h_places{a}", align_bytes=ALIGN) for a in range(2)]
         for a in range(2):
-            cols = slice(a * half, (a + 1) * half)
+            notes = slice(a * HALF, (a + 1) * HALF)
             for t in range(PLACES):
                 nc.tensor.matmul_mx(
-                    out=h_banks[t][:, cols],
+                    out=h_banks[t][:, notes],
                     lhsT=wb_wd[:, 2 * P * t : 2 * P * (t + 1)].bitcast(FP4X4),
                     lhsT_scale=wb_sd[:, P * t : P * (t + 1)],
-                    rhs=note_wg[:, cols].bitcast(FP8X4),
-                    rhs_scale=note_sg[:, cols],
+                    rhs=note_wg[:, notes].bitcast(FP8X4),
+                    rhs_scale=note_sg[:, notes],
                     start=True,
                     stop=True,
                 )
-                nc.scalar.activation(h_planes[:, t, cols], h_banks[t][:, cols], ACT.Copy, scale=factor[:, t : t + 1])
+                nc.scalar.activation(h_places[a][:, t, :], h_banks[t][:, notes], ACT.Copy, scale=factor[:, t : t + 1])
         for a in range(2):
-            cols = slice(a * half, (a + 1) * half)
-            words = slice(a * half * PLACES, (a + 1) * half * PLACES)
+            values = slice(a * HALF * PLACES, (a + 1) * HALF * PLACES)
             nc.vector.tensor_copy(
-                h_bf[:, words].rearrange("p (c i t) -> p c t i", i=4, t=PLACES),
-                h_planes[:, :, cols].rearrange("p t (c i) -> p c t i", i=4),
+                h_bf[:, values].rearrange("p (c i t) -> p c t i", i=LINE, t=PLACES),
+                h_places[a][:].rearrange("p t (c i) -> p c t i", i=LINE),
             )
         for a in range(2):
-            cols = slice(a * half, (a + 1) * half)
-            words = slice(a * half * PLACES, (a + 1) * half * PLACES)
-            nc.vector.quantize_mx(out=h_q[:, cols].bitcast(FP8X4), scales=h_qs[:, cols], in_=h_bf[:, words])
+            notes = slice(a * HALF, (a + 1) * HALF)
+            values = slice(a * HALF * PLACES, (a + 1) * HALF * PLACES)
+            nc.vector.quantize_mx(out=h_q[:, notes].bitcast(FP8X4), scales=h_qs[:, notes], in_=h_bf[:, values])
 
         z_bf = []
-        for c in range(CHUNKS):
-            cols = slice(c * CHUNK, (c + 1) * CHUNK)
-            bank = ps.tile([P, PLACES * CHUNK], F32, name="z_bank", tag=f"z{c}")
+        for c in range(TILES):
+            pages = slice(c * P, (c + 1) * P)
+            z_bank = ps.tile([P, PLACES * P], F32, name="z_bank", tag=f"z{c}")
             for t in range(PLACES):
                 nc.tensor.matmul_mx(
-                    out=bank[:, t * CHUNK : (t + 1) * CHUNK],
+                    out=z_bank[:, t * P : (t + 1) * P],
                     lhsT=wa_wd[:, P * t : P * (t + 1)].bitcast(FP8X4),
                     lhsT_scale=wa_sd[:, P * t : P * (t + 1)],
-                    rhs=page_wg[:, cols].bitcast(FP4X4),
-                    rhs_scale=page_sg[:, cols],
+                    rhs=page_wg[:, pages].bitcast(FP4X4),
+                    rhs_scale=page_sg[:, pages],
                     start=True,
                     stop=True,
                 )
-            zc = sb.tile([P, CHUNK * PLACES], BF16, name=f"z_bf{c}", tag=f"z_then_table{c}", align_bytes=64)
+            z_tile = sb.tile([P, P * PLACES], BF16, name=f"z_bf{c}", tag=f"z_bf_then_table{c}", align_bytes=ALIGN)
             nc.scalar.activation(
-                zc[:].rearrange("p (n t) -> p n t", t=PLACES),
-                bank[:].rearrange("p (t n) -> p n t", t=PLACES),
+                z_tile[:].rearrange("p (n t) -> p n t", t=PLACES),
+                z_bank[:].rearrange("p (t n) -> p n t", t=PLACES),
                 ACT.Copy,
             )
-            z_bf.append(zc)
+            z_bf.append(z_tile)
 
         z_mx = []
-        for c in range(CHUNKS):
-            z_q = sb.tile([P, CHUNK], U32, name=f"z_q{c}", align_bytes=64)
-            z_qs = sb.tile([P, CHUNK], U8, name=f"z_qs{c}", align_bytes=64)
+        for c in range(TILES):
+            z_q = sb.tile([P, P], U32, name=f"z_q{c}", align_bytes=ALIGN)
+            z_qs = sb.tile([P, P], U8, name=f"z_qs{c}", align_bytes=ALIGN)
             nc.vector.quantize_mx(out=z_q[:].bitcast(FP8X4), scales=z_qs[:], in_=z_bf[c][:])
             z_mx.append((z_q, z_qs))
 
-        for c in range(CHUNKS):
+        for c in range(TILES):
             z_q, z_qs = z_mx[c]
-            bank = ps.tile([P, J], F32, name="s_bank", tag=f"hs{c}")
+            s_bank = ps.tile([P, J], F32, name="s_bank", tag=f"h_then_s{c}")
             nc.tensor.matmul_mx(
-                out=bank[:],
+                out=s_bank[:],
                 lhsT=z_q[:].bitcast(FP8X4),
                 lhsT_scale=z_qs[:],
                 rhs=h_q[:].bitcast(FP8X4),
@@ -177,11 +182,11 @@ def tile_attend_matchtable_kernel(
                 start=True,
                 stop=True,
             )
-            table = sb.tile([P, J], F32, name=f"table{c}", tag=f"z_then_table{CHUNKS - 1 - c}", align_bytes=64)
+            table = sb.tile([P, J], F32, name=f"table{c}", tag=f"z_bf_then_table{(c + 1) % TILES}", align_bytes=ALIGN)
             top = sb.tile([P, 1], F32, name=f"top{c}")
             neg_top = sb.tile([P, 1], F32, name=f"neg_top{c}")
             picked = sb.tile([P, C], F32, name=f"picked{c}")
-            nc.vector.tensor_scalar(table[:], bank[:], 1.0, None, ALU.mult, ALU.max, accum_out=top[:])
+            nc.vector.tensor_scalar(table[:], s_bank[:], 1.0, None, ALU.mult, ALU.max, accum_out=top[:])
             nc.gpsimd.tensor_scalar(neg_top[:], top[:], -1.0, 0.0, ALU.mult, ALU.add)
             nc.scalar.activation(picked[:], table[:].indirect(col_list[:]), ACT.Exp, bias=neg_top[:])
             nc.sync.dma_start(out=out[c * P : (c + 1) * P, :], in_=picked[:])

@@ -20,26 +20,28 @@ ACT = mybir.ActivationFunctionType
 P = 128
 PLACES = 4
 RUN = 8
-BLOCKS = K // (PLACES * RUN)
+K_BLOCKS = K // (PLACES * RUN)
+D_BLOCKS = D // (PLACES * RUN)
 QUADRANT = 32
 SCALE_ROWS = 4
 LIST_ROWS = 16
 TILES = I // P
-HALF = J // 2
+HALVES = 2
+HALF = J // HALVES
 LINE = 4
 ALIGN = 64
 
 
-def load_scale_rows(nc, scale_tile, scales):
+def load_scale_rows(queues, scale_tile, scales):
     rows = scales[0].bitcast(I32)
     for r in range(SCALE_ROWS):
-        nc.sync.dma_start(out=scale_tile[r:P:QUADRANT, :].bitcast(I32), in_=rows[r:BLOCKS:SCALE_ROWS, :])
+        queues[r].dma_start(out=scale_tile[r:P:QUADRANT, :].bitcast(I32), in_=rows[r:D_BLOCKS:SCALE_ROWS, :])
 
 
-def dealt_views(dealt, natural, dtype):
-    return (
-        dealt[:].bitcast(dtype).rearrange("p (t g r) -> p t g r", t=PLACES, g=BLOCKS),
-        natural[:].bitcast(dtype).rearrange("p (g t r) -> p t g r", t=PLACES, g=BLOCKS),
+def deal_columns(nc, dealt, natural):
+    nc.scalar.copy(
+        dealt[:].bitcast(U32).rearrange("p (t g r) -> p t g r", t=PLACES, g=K_BLOCKS),
+        natural[:].bitcast(U32).rearrange("p (g t r) -> p t g r", t=PLACES, g=K_BLOCKS),
     )
 
 
@@ -59,7 +61,7 @@ def tile_attend_matchtable_kernel(
         note_w = sb.tile([P, U], U32, name="note_w", align_bytes=ALIGN)
         note_s = sb.tile([P, U], U8, name="note_s", align_bytes=ALIGN)
         wa_w = sb.tile([P, K], U32, name="wa_w", align_bytes=ALIGN)
-        wa_s = sb.tile([P, K], U8, name="wa_s", tag="wa_s_then_h_q", align_bytes=ALIGN)
+        wa_s = sb.tile([P, K], U8, name="wa_s", tag="wa_s_then_places", align_bytes=ALIGN)
         wb_w = sb.tile([P, 2 * K], U8, name="wb_w", align_bytes=ALIGN)
         wb_s = sb.tile([P, K], U8, name="wb_s", align_bytes=ALIGN)
         factor = sb.tile([P, PLACES], F32, name="factor")
@@ -72,21 +74,22 @@ def tile_attend_matchtable_kernel(
         nc.vector.memset(page_s[:].bitcast(I32), 0)
         nc.vector.memset(wa_s[:].bitcast(I32), 0)
 
+        on_sync = [nc.sync] * SCALE_ROWS
         nc.gpsimd.dma_start(out=wb_w[:].bitcast(I32), in_=wb_words[0].bitcast(I32))
         nc.gpsimd.dma_start(out=wa_w[:].bitcast(I32), in_=wa_words[0].rearrange("p n t -> p (n t)").bitcast(I32))
         make_identity(nc, identity[:])
         nc.sync.dma_start(note_list[:], offs2)
         nc.sync.dma_start(out=note_w[:].bitcast(I32), in_=notes_words[0].rearrange("p n t -> p (n t)").bitcast(I32))
-        load_scale_rows(nc, note_s, notes_scales)
+        load_scale_rows(on_sync, note_s, notes_scales)
         nc.sync.dma_start(page_list[:], offs)
         nc.sync.dma_start(out=page_w[:].bitcast(I32), in_=pages_words[0].bitcast(I32))
         nc.sync.dma_start(
             out=factor_rows[0:PLACES, :].rearrange("t (g r) -> t g r", r=RUN),
             in_=kf.rearrange("(g t r) o -> t g (r o)", t=PLACES, r=RUN),
         )
-        load_scale_rows(nc, wb_s, wb_scales)
-        load_scale_rows(nc, page_s, pages_scales)
-        load_scale_rows(nc, wa_s, wa_scales)
+        load_scale_rows(on_sync, wb_s, wb_scales)
+        load_scale_rows(on_sync, page_s, pages_scales)
+        load_scale_rows(on_sync[:-1] + [nc.gpsimd], wa_s, wa_scales)
         nc.sync.dma_start(col_list[:], offs3)
 
         factor_bank = ps.tile([P, PLACES * P], F32, name="factor_bank", tag=f"z{TILES - 1}")
@@ -97,9 +100,10 @@ def tile_attend_matchtable_kernel(
         wb_sd = sb.tile([P, K], U8, name="wb_sd", align_bytes=ALIGN)
         wa_wd = sb.tile([P, K], U32, name="wa_wd", align_bytes=ALIGN)
         wa_sd = sb.tile([P, K], U8, name="wa_sd", align_bytes=ALIGN)
-        nc.scalar.copy(*dealt_views(wb_wd, wb_w, U32))
-        nc.scalar.copy(*dealt_views(wa_wd, wa_w, U32))
-        nc.scalar.copy(*dealt_views(wb_sd, wb_s, U32))
+        deal_columns(nc, wb_wd, wb_w)
+        deal_columns(nc, wa_wd, wa_w)
+        deal_columns(nc, wb_sd, wb_s)
+        deal_columns(nc, wa_sd, wa_s)
 
         note_wg = sb.tile([P, J], U32, name="note_wg", align_bytes=ALIGN)
         note_sg = sb.tile([P, J], U8, name="note_sg", align_bytes=ALIGN)
@@ -110,14 +114,15 @@ def tile_attend_matchtable_kernel(
         nc.vector.tensor_copy(page_wg[:], page_w[:].indirect(page_list[:]))
         nc.vector.tensor_copy(page_sg[:], page_s[:].indirect(page_list[:]))
 
-        nc.vector.tensor_copy(*dealt_views(wa_sd, wa_s, I32))
-
         h_bf = sb.tile([P, J * PLACES], BF16, name="h_bf", tag="page_s_then_h_bf", align_bytes=ALIGN)
-        h_q = sb.tile([P, J], U32, name="h_q", tag="wa_s_then_h_q", align_bytes=ALIGN)
+        h_q = sb.tile([P, J], U32, name="h_q", align_bytes=ALIGN)
         h_qs = sb.tile([P, J], U8, name="h_qs", align_bytes=ALIGN)
         h_banks = [ps.tile([P, J], F32, name="h_bank", tag=f"h_then_s{t}") for t in range(PLACES)]
-        h_places = [sb.tile([P, PLACES, HALF], BF16, name=f"h_places{a}", align_bytes=ALIGN) for a in range(2)]
-        for a in range(2):
+        h_places = [
+            sb.tile([P, PLACES, HALF], BF16, name="h_places0", align_bytes=ALIGN),
+            sb.tile([P, PLACES, HALF], BF16, name="h_places1", tag="wa_s_then_places", align_bytes=ALIGN),
+        ]
+        for a in range(HALVES):
             notes = slice(a * HALF, (a + 1) * HALF)
             for t in range(PLACES):
                 nc.tensor.matmul_mx(
@@ -130,13 +135,13 @@ def tile_attend_matchtable_kernel(
                     stop=True,
                 )
                 nc.scalar.activation(h_places[a][:, t, :], h_banks[t][:, notes], ACT.Copy, scale=factor[:, t : t + 1])
-        for a in range(2):
+        for a in range(HALVES):
             values = slice(a * HALF * PLACES, (a + 1) * HALF * PLACES)
             nc.vector.tensor_copy(
                 h_bf[:, values].rearrange("p (c i t) -> p c t i", i=LINE, t=PLACES),
                 h_places[a][:].rearrange("p t (c i) -> p c t i", i=LINE),
             )
-        for a in range(2):
+        for a in range(HALVES):
             notes = slice(a * HALF, (a + 1) * HALF)
             values = slice(a * HALF * PLACES, (a + 1) * HALF * PLACES)
             nc.vector.quantize_mx(out=h_q[:, notes].bitcast(FP8X4), scales=h_qs[:, notes], in_=h_bf[:, values])

from contextlib import ExitStack

import concourse.mybir as mybir
from concourse.masks import make_identity

D, K, T, U, I, J, C = 512, 512, 2048, 1024, 512, 512, 256
FLOPS = 2 * D * K * I + 2 * D * K * J + 2 * K * I * J

F32 = mybir.dt.float32
BF16 = mybir.dt.bfloat16
I32 = mybir.dt.int32
U32 = mybir.dt.uint32
U16 = mybir.dt.uint16
U8 = mybir.dt.uint8
FP8X4 = mybir.dt.float8_e4m3fn_x4
FP4X4 = mybir.dt.float4_e2m1fn_x4
ALU = mybir.AluOpType
ACT = mybir.ActivationFunctionType

P = 128
PLACES = 4
RUN = 8
K_BLOCKS = K // (PLACES * RUN)
D_BLOCKS = D // (PLACES * RUN)
QUADRANT = 32
SCALE_ROWS = 4
LIST_ROWS = 16
TILES = I // P
HALVES = 2
HALF = J // HALVES
LINE = 4
ALIGN = 64


def load_scale_rows(queues, scale_tile, scales):
    rows = scales[0].bitcast(I32)
    for r in range(SCALE_ROWS):
        queues[r].dma_start(out=scale_tile[r:P:QUADRANT, :].bitcast(I32), in_=rows[r:D_BLOCKS:SCALE_ROWS, :])


def deal_columns(nc, dealt, natural):
    nc.scalar.copy(
        dealt[:].bitcast(U32).rearrange("p (t g r) -> p t g r", t=PLACES, g=K_BLOCKS),
        natural[:].bitcast(U32).rearrange("p (g t r) -> p t g r", t=PLACES, g=K_BLOCKS),
    )


def tile_attend_matchtable_kernel(
    tc, pages_words, pages_scales, wa_words, wa_scales, notes_words, notes_scales, wb_words, wb_scales, kf, offs, offs2, offs3, out
):
    nc = tc.nc
    with ExitStack() as ctx:
        sb = ctx.enter_context(tc.tile_pool(name="sb", bufs=1))
        ps = ctx.enter_context(tc.psum_pool(name="ps", bufs=1))

        page_list = sb.tile([P, I // LIST_ROWS], U16, name="page_list")
        note_list = sb.tile([P, J // LIST_ROWS], U16, name="note_list")
        col_list = sb.tile([P, C // LIST_ROWS], U16, name="col_list")
        page_w = sb.tile([P, T], U16, name="page_w", align_bytes=ALIGN)
        page_s = sb.tile([P, T], U8, name="page_s", tag="page_s_then_h_bf", align_bytes=ALIGN)
        note_w = sb.tile([P, U], U32, name="note_w", align_bytes=ALIGN)
        note_s = sb.tile([P, U], U8, name="note_s", align_bytes=ALIGN)
        wa_w = sb.tile([P, K], U32, name="wa_w", align_bytes=ALIGN)
        wa_s = sb.tile([P, K], U8, name="wa_s", tag="wa_s_then_places", align_bytes=ALIGN)
        wb_w = sb.tile([P, 2 * K], U8, name="wb_w", align_bytes=ALIGN)
        wb_s = sb.tile([P, K], U8, name="wb_s", align_bytes=ALIGN)
        factor = sb.tile([P, PLACES], F32, name="factor")
        factor_rows = sb.tile([P, P], F32, name="factor_rows")
        identity = sb.tile([P, P], F32, name="identity")

        nc.vector.memset(note_s[:].bitcast(I32), 0)
        nc.vector.memset(factor_rows[:], 0.0)
        nc.vector.memset(wb_s[:].bitcast(I32), 0)
        nc.vector.memset(page_s[:].bitcast(I32), 0)
        nc.vector.memset(wa_s[:].bitcast(I32), 0)

        on_sync = [nc.sync] * SCALE_ROWS
        nc.gpsimd.dma_start(out=wb_w[:].bitcast(I32), in_=wb_words[0].bitcast(I32))
        nc.gpsimd.dma_start(out=wa_w[:].bitcast(I32), in_=wa_words[0].rearrange("p n t -> p (n t)").bitcast(I32))
        make_identity(nc, identity[:])
        nc.sync.dma_start(note_list[:], offs2)
        nc.sync.dma_start(out=note_w[:].bitcast(I32), in_=notes_words[0].rearrange("p n t -> p (n t)").bitcast(I32))
        load_scale_rows(on_sync, note_s, notes_scales)
        nc.sync.dma_start(page_list[:], offs)
        nc.sync.dma_start(out=page_w[:].bitcast(I32), in_=pages_words[0].bitcast(I32))
        nc.sync.dma_start(
            out=factor_rows[0:PLACES, :].rearrange("t (g r) -> t g r", r=RUN),
            in_=kf.rearrange("(g t r) o -> t g (r o)", t=PLACES, r=RUN),
        )
        load_scale_rows(on_sync, wb_s, wb_scales)
        load_scale_rows(on_sync, page_s, pages_scales)
        load_scale_rows(on_sync[:-1] + [nc.gpsimd], wa_s, wa_scales)
        nc.sync.dma_start(col_list[:], offs3)

        factor_bank = ps.tile([P, PLACES * P], F32, name="factor_bank", tag=f"z{TILES - 1}")
        nc.tensor.transpose(factor_bank[:, 0:P], factor_rows[:], identity[:])
        nc.scalar.copy(factor[:], factor_bank[:, 0:PLACES])

        wb_wd = sb.tile([P, 2 * K], U8, name="wb_wd", align_bytes=ALIGN)
        wb_sd = sb.tile([P, K], U8, name="wb_sd", align_bytes=ALIGN)
        wa_wd = sb.tile([P, K], U32, name="wa_wd", align_bytes=ALIGN)
        wa_sd = sb.tile([P, K], U8, name="wa_sd", align_bytes=ALIGN)
        deal_columns(nc, wb_wd, wb_w)
        deal_columns(nc, wa_wd, wa_w)
        deal_columns(nc, wb_sd, wb_s)
        deal_columns(nc, wa_sd, wa_s)

        note_wg = sb.tile([P, J], U32, name="note_wg", align_bytes=ALIGN)
        note_sg = sb.tile([P, J], U8, name="note_sg", align_bytes=ALIGN)
        page_wg = sb.tile([P, I], U16, name="page_wg", align_bytes=ALIGN)
        page_sg = sb.tile([P, I], U8, name="page_sg", align_bytes=ALIGN)
        nc.vector.tensor_copy(note_wg[:], note_w[:].indirect(note_list[:]))
        nc.vector.tensor_copy(note_sg[:], note_s[:].indirect(note_list[:]))
        nc.vector.tensor_copy(page_wg[:], page_w[:].indirect(page_list[:]))
        nc.vector.tensor_copy(page_sg[:], page_s[:].indirect(page_list[:]))

        h_bf = sb.tile([P, J * PLACES], BF16, name="h_bf", tag="page_s_then_h_bf", align_bytes=ALIGN)
        h_q = sb.tile([P, J], U32, name="h_q", align_bytes=ALIGN)
        h_qs = sb.tile([P, J], U8, name="h_qs", align_bytes=ALIGN)
        h_banks = [ps.tile([P, J], F32, name="h_bank", tag=f"h_then_s{t}") for t in range(PLACES)]
        h_places = [
            sb.tile([P, PLACES, HALF], BF16, name="h_places0", align_bytes=ALIGN),
            sb.tile([P, PLACES, HALF], BF16, name="h_places1", tag="wa_s_then_places", align_bytes=ALIGN),
        ]
        for a in range(HALVES):
            notes = slice(a * HALF, (a + 1) * HALF)
            for t in range(PLACES):
                nc.tensor.matmul_mx(
                    out=h_banks[t][:, notes],
                    lhsT=wb_wd[:, 2 * P * t : 2 * P * (t + 1)].bitcast(FP4X4),
                    lhsT_scale=wb_sd[:, P * t : P * (t + 1)],
                    rhs=note_wg[:, notes].bitcast(FP8X4),
                    rhs_scale=note_sg[:, notes],
                    start=True,
                    stop=True,
                )
                nc.scalar.activation(h_places[a][:, t, :], h_banks[t][:, notes], ACT.Copy, scale=factor[:, t : t + 1])
        for a in range(HALVES):
            values = slice(a * HALF * PLACES, (a + 1) * HALF * PLACES)
            nc.vector.tensor_copy(
                h_bf[:, values].rearrange("p (c i t) -> p c t i", i=LINE, t=PLACES),
                h_places[a][:].rearrange("p t (c i) -> p c t i", i=LINE),
            )
        for a in range(HALVES):
            notes = slice(a * HALF, (a + 1) * HALF)
            values = slice(a * HALF * PLACES, (a + 1) * HALF * PLACES)
            nc.vector.quantize_mx(out=h_q[:, notes].bitcast(FP8X4), scales=h_qs[:, notes], in_=h_bf[:, values])

        z_bf = []
        for c in range(TILES):
            pages = slice(c * P, (c + 1) * P)
            z_bank = ps.tile([P, PLACES * P], F32, name="z_bank", tag=f"z{c}")
            for t in range(PLACES):
                nc.tensor.matmul_mx(
                    out=z_bank[:, t * P : (t + 1) * P],
                    lhsT=wa_wd[:, P * t : P * (t + 1)].bitcast(FP8X4),
                    lhsT_scale=wa_sd[:, P * t : P * (t + 1)],
                    rhs=page_wg[:, pages].bitcast(FP4X4),
                    rhs_scale=page_sg[:, pages],
                    start=True,
                    stop=True,
                )
            z_tile = sb.tile([P, P * PLACES], BF16, name=f"z_bf{c}", tag=f"z_bf_then_table{c}", align_bytes=ALIGN)
            nc.scalar.activation(
                z_tile[:].rearrange("p (n t) -> p n t", t=PLACES),
                z_bank[:].rearrange("p (t n) -> p n t", t=PLACES),
                ACT.Copy,
            )
            z_bf.append(z_tile)

        z_mx = []
        for c in range(TILES):
            z_q = sb.tile([P, P], U32, name=f"z_q{c}", align_bytes=ALIGN)
            z_qs = sb.tile([P, P], U8, name=f"z_qs{c}", align_bytes=ALIGN)
            nc.vector.quantize_mx(out=z_q[:].bitcast(FP8X4), scales=z_qs[:], in_=z_bf[c][:])
            z_mx.append((z_q, z_qs))

        for c in range(TILES):
            z_q, z_qs = z_mx[c]
            s_bank = ps.tile([P, J], F32, name="s_bank", tag=f"h_then_s{c}")
            nc.tensor.matmul_mx(
                out=s_bank[:],
                lhsT=z_q[:].bitcast(FP8X4),
                lhsT_scale=z_qs[:],
                rhs=h_q[:].bitcast(FP8X4),
                rhs_scale=h_qs[:],
                start=True,
                stop=True,
            )
            table = sb.tile([P, J], F32, name=f"table{c}", tag=f"z_bf_then_table{(c + 1) % TILES}", align_bytes=ALIGN)
            top = sb.tile([P, 1], F32, name=f"top{c}")
            neg_top = sb.tile([P, 1], F32, name=f"neg_top{c}")
            picked = sb.tile([P, C], F32, name=f"picked{c}")
            nc.vector.tensor_scalar(table[:], s_bank[:], 1.0, None, ALU.mult, ALU.max, accum_out=top[:])
            nc.gpsimd.tensor_scalar(neg_top[:], top[:], -1.0, 0.0, ALU.mult, ALU.add)
            nc.scalar.activation(picked[:], table[:].indirect(col_list[:]), ACT.Exp, bias=neg_top[:])
            nc.sync.dma_start(out=out[c * P : (c + 1) * P, :], in_=picked[:])
